import numpy as np, ml_dtypes
CORES = [6,14,30,38,62,70,86,94,102]
N = 9
F = 32
def setup_inputs(rng):
    m = (rng.standard_normal((N, 128, 128), dtype=np.float32) / 11).astype(ml_dtypes.bfloat16)
    return {"m": m, "mt": m.transpose(0, 2, 1).copy(), "x": rng.standard_normal((N, 128, F), dtype=np.float32).astype(ml_dtypes.bfloat16)}
def setup_inputs_big(rng):
    d = setup_inputs(rng)
    for k in ("x",): d[k] = (d[k].astype(np.float32) * 1048576.0).astype(d[k].dtype)
    return d
def setup_inputs_small(rng):
    d = setup_inputs(rng)
    for k in ("x",): d[k] = (d[k].astype(np.float32) * (1 / 1048576.0)).astype(d[k].dtype)
    return d
def setup_inputs_apart(rng):
    d = setup_inputs(rng)
    f = (10.0 ** rng.permutation(np.linspace(-1.5, 1.5, N))).astype(np.float32).reshape(N, 1, 1)
    for k in ("x",): d[k] = (d[k].astype(np.float32) * f).astype(d[k].dtype)
    return d
def reference(m, mt, x):
    M, X = m.astype(np.float64), x.astype(np.float64)
    y = np.zeros((N, 128, F)); p = X[0]
    for r in range(N):
        p = M[r].T @ p
        y[r] = p
    return {"y": y.astype(ml_dtypes.bfloat16)}

@@ -1,0 +1,210 @@
+from concourse.bass import DstId, RemoteDMATransfer
+
+N = 9
+P = 128
+F = 32
+
+SRC = [None, 0, 0, 0, 0, 0, 0, 0, 0]
+FIRST = []
+NE_M = 8
+NE_P = 8
+WM, WP, SB, SS, HOP = 1.0, 0.8, 0.5, 0.4, 3.0
+
+
+def _chain(a, b):
+    return (b,) if a == b else ((a,), _chain(a + 1, b))
+
+
+SEGS = [None] + [[_chain(SRC[r] + 1, r)] for r in range(1, N)]
+
+
+def _key(r):
+    return (0 if r in FIRST else 1, r)
+
+
+def _make_plan():
+    form = {}
+    ops = []
+    for r in range(N):
+        lst = []
+
+        def node(t, tr):
+            if len(t) == 1:
+                if t[0] == r:
+                    return ("own",)
+                form[(t[0], r)] = "t" if tr else "m"
+                return ("land", t[0])
+            left = node(t[0], True)
+            right = node(t[1], False)
+            lst.append((right, left, P) if tr else (left, right, P))
+            return ("op", len(lst) - 1)
+
+        if r == 0:
+            lst.append((("own",), ("x",), F))
+        else:
+            v = ("pin",)
+            for seg in SEGS[r]:
+                u = node(seg, False)
+                lst.append((u, v, F))
+                v = ("op", len(lst) - 1)
+        ops.append(lst)
+    mcalls = []
+    arr_m = {}
+    free = []
+    for k in range(N):
+        dests = sorted([r for r in range(k + 1, N) if (k, r) in form], key=_key)
+        calls = []
+        t = 0.0
+        for r in dests:
+            if calls and calls[-1][0] == form[(k, r)]:
+                calls[-1][1].append(r)
+            else:
+                calls.append((form[(k, r)], [r]))
+            t += WM
+            arr_m[(k, r)] = t
+        mcalls.append(calls)
+        free.append(t)
+    pdests = [sorted([r for r in range(1, N) if SRC[r] == j], key=_key) for j in range(N)]
+    arr_p = {}
+    order = []
+    for r in range(N):
+        lst = ops[r]
+        start = [0.0] * len(lst)
+        end = [0.0] * len(lst)
+        for i, (a, b, cols) in enumerate(lst):
+            t = 0.0
+            for d in (a, b):
+                if d[0] == "land":
+                    t = max(t, arr_m[(d[1], r)])
+                elif d[0] == "pin":
+                    t = max(t, arr_p[r])
+                elif d[0] == "op":
+                    t = max(t, end[d[1]])
+            start[i] = t
+            end[i] = t + (SB if cols == P else SS)
+        order.append(sorted(range(len(lst)), key=lambda i: (start[i], i)))
+        t = max(end[-1] + (HOP if r else 0.0), free[r])
+        for d in pdests[r]:
+            t += WP
+            arr_p[d] = t
+    return ops, order, mcalls, pdests
+
+
+OPS, ORDER, MCALLS, PDESTS = _make_plan()
+MAXOPS = max(len(o) for o in OPS)
+
+SCRATCH = {
+    "own_m": ("sbuf", [P, P], "bfloat16"),
+    "own_t": ("sbuf", [P, P], "bfloat16"),
+    "xs": ("sbuf", [P, F], "bfloat16"),
+    "pin": ("sbuf", [P, F], "bfloat16"),
+    "yb": ("sbuf", [P, F], "bfloat16"),
+}
+SEMAPHORES = ["ldm", "ldt", "ldx", "arp", "sent", "st"]
+for _k in range(1, N - 1):
+    SCRATCH["land%d" % _k] = ("sbuf", [P, P], "bfloat16")
+    SEMAPHORES.append("arr%d" % _k)
+for _i in range(MAXOPS):
+    SCRATCH["u%d" % _i] = ("sbuf", [P, P], "bfloat16")
+    SCRATCH["ps%d" % _i] = ("psum", [P, 512], "float32")
+    SEMAPHORES.append("mm%d" % _i)
+    SEMAPHORES.append("cp%d" % _i)
+
+
+def _engines(topo, cores, src, dests, want):
+    allowed = -1
+    for d in dests:
+        if not topo.may_write(cores[src], cores[d]):
+            raise ValueError("rank %d may not write to rank %d" % (src, d))
+        allowed &= topo.mask(cores[src], cores[d])
+    mask = 0
+    n = 0
+    b = 0
+    while n < want and (allowed >> b):
+        if (allowed >> b) & 1:
+            mask |= 1 << b
+            n += 1
+        b += 1
+    return mask, n
+
+
+def _send(g, T, topo, src, dests, want, buf, land, sem):
+    mask, n = _engines(topo, T.cores, src, dests, want)
+    ids = []
+    for d in dests:
+        rid, pid, _se = topo.addr(T.cores[d])
+        ids.append(DstId(rid=rid, pnc=pid))
+    g.remote_dma_fused(
+        [RemoteDMATransfer(dst_ids=ids, dma_engine_mask=mask, remote_sem=sem,
+                           srcs=[buf[:]], dsts=[land[:] for _d in dests], alu_op=0)],
+        local_sem=T.sem.sent)
+    return n
+
+
+def rank_program(g, core, T, topo):
+    r = T.rank_of(core)
+    if r is None:
+        return
+    sem = T.sem
+    forms_sent = [c[0] for c in MCALLS[r]]
+
+    if r == 0:
+        g.sync.dma_start(T.xs[:], T.x[:]).then_inc(sem.ldx, 16)
+    elif "t" in forms_sent:
+        g.sync.dma_start(T.own_t[:], T.mt[:]).then_inc(sem.ldt, 16)
+    g.scalar.dma_start(T.own_m[:], T.m[:]).then_inc(sem.ldm, 16)
+
+    sent = 0
+    waited = []
+    for fm, dests in MCALLS[r]:
+        if fm not in waited:
+            g.wait_ge(sem.ldt if fm == "t" else sem.ldm, 16)
+            waited.append(fm)
+        sent += _send(g, T, topo, r, dests, NE_M, T.own_t if fm == "t" else T.own_m,
+                      T["land%d" % r], sem["arr%d" % r])
+
+    lst = OPS[r]
+    last = len(lst) - 1
+
+    def out_of(i):
+        if i == last:
+            return T.yb[:]
+        return T["u%d" % i][:, 0:lst[i][2]]
+
+    def operand(d):
+        if d[0] == "own":
+            g.tensor.wait_ge(sem.ldm, 16)
+            return T.own_m[:]
+        if d[0] == "x":
+            g.tensor.wait_ge(sem.ldx, 16)
+            return T.xs[:]
+        if d[0] == "pin":
+            j = SRC[r]
+            g.tensor.wait_ge(sem.arp, _engines(topo, T.cores, j, PDESTS[j], NE_P)[1])
+            return T.pin[:]
+        if d[0] == "land":
+            k = d[1]
+            for _fm, dests in MCALLS[k]:
+                if r in dests:
+                    g.tensor.wait_ge(sem["arr%d" % k], _engines(topo, T.cores, k, dests, NE_M)[1])
+            return T["land%d" % k][:]
+        g.tensor.wait_ge(sem["cp%d" % d[1]], 1)
+        return out_of(d[1])
+
+    for i in ORDER[r]:
+        a, b, cols = lst[i]
+        lhs = operand(a)
+        rhs = operand(b)
+        ps = T["ps%d" % i][:, 0:cols]
+        g.tensor.matmul(ps, lhs, rhs, start=True, stop=True).then_inc(sem["mm%d" % i], 1)
+        g.vector.wait_ge(sem["mm%d" % i], 1)
+        g.vector.tensor_copy(out_of(i), ps).then_inc(sem["cp%d" % i], 1)
+
+    g.sync.wait_ge(sem["cp%d" % last], 1)
+    g.sync.dma_start(T.y[:], T.yb[:]).then_inc(sem.st, 16)
+    if PDESTS[r]:
+        g.wait_ge(sem["cp%d" % last], 1)
+        sent += _send(g, T, topo, r, PDESTS[r], NE_P, T.yb, T.pin, sem.arp)
+    if sent:
+        g.wait_ge(sem.sent, sent)
+    g.sync.wait_ge(sem.st, 16)

@@ -11,11 +11,15 @@ NE_P = 8
 WM, WP, SB, SS, HOP = 1.0, 0.8, 0.5, 0.4, 3.0
 
 
-def _chain(a, b):
-    return (b,) if a == b else ((a,), _chain(a + 1, b))
+def _pairs(a, b):
+    items = [((k,), (k + 1,)) if k < b else (k,) for k in range(a, b + 1, 2)]
+    t = items[-1]
+    for it in reversed(items[:-1]):
+        t = (it, t)
+    return t
 
 
-SEGS = [None] + [[_chain(SRC[r] + 1, r)] for r in range(1, N)]
+SEGS = [None] + [([(SRC[r] + 1,)] + ([_pairs(SRC[r] + 2, r)] if r > SRC[r] + 1 else [])) for r in range(1, N)]
 
 
 def _key(r):

from concourse.bass import DstId, RemoteDMATransfer

N = 9
P = 128
F = 32

SRC = [None, 0, 0, 0, 0, 0, 0, 0, 0]
FIRST = []
NE_M = 8
NE_P = 8
WM, WP, SB, SS, HOP = 1.0, 0.8, 0.5, 0.4, 3.0


def _pairs(a, b):
    items = [((k,), (k + 1,)) if k < b else (k,) for k in range(a, b + 1, 2)]
    t = items[-1]
    for it in reversed(items[:-1]):
        t = (it, t)
    return t


SEGS = [None] + [([(SRC[r] + 1,)] + ([_pairs(SRC[r] + 2, r)] if r > SRC[r] + 1 else [])) for r in range(1, N)]


def _key(r):
    return (0 if r in FIRST else 1, r)


def _make_plan():
    form = {}
    ops = []
    for r in range(N):
        lst = []

        def node(t, tr):
            if len(t) == 1:
                if t[0] == r:
                    return ("own",)
                form[(t[0], r)] = "t" if tr else "m"
                return ("land", t[0])
            left = node(t[0], True)
            right = node(t[1], False)
            lst.append((right, left, P) if tr else (left, right, P))
            return ("op", len(lst) - 1)

        if r == 0:
            lst.append((("own",), ("x",), F))
        else:
            v = ("pin",)
            for seg in SEGS[r]:
                u = node(seg, False)
                lst.append((u, v, F))
                v = ("op", len(lst) - 1)
        ops.append(lst)
    mcalls = []
    arr_m = {}
    free = []
    for k in range(N):
        dests = sorted([r for r in range(k + 1, N) if (k, r) in form], key=_key)
        calls = []
        t = 0.0
        for r in dests:
            if calls and calls[-1][0] == form[(k, r)]:
                calls[-1][1].append(r)
            else:
                calls.append((form[(k, r)], [r]))
            t += WM
            arr_m[(k, r)] = t
        mcalls.append(calls)
        free.append(t)
    pdests = [sorted([r for r in range(1, N) if SRC[r] == j], key=_key) for j in range(N)]
    arr_p = {}
    order = []
    for r in range(N):
        lst = ops[r]
        start = [0.0] * len(lst)
        end = [0.0] * len(lst)
        for i, (a, b, cols) in enumerate(lst):
            t = 0.0
            for d in (a, b):
                if d[0] == "land":
                    t = max(t, arr_m[(d[1], r)])
                elif d[0] == "pin":
                    t = max(t, arr_p[r])
                elif d[0] == "op":
                    t = max(t, end[d[1]])
            start[i] = t
            end[i] = t + (SB if cols == P else SS)
        order.append(sorted(range(len(lst)), key=lambda i: (start[i], i)))
        t = max(end[-1] + (HOP if r else 0.0), free[r])
        for d in pdests[r]:
            t += WP
            arr_p[d] = t
    return ops, order, mcalls, pdests


OPS, ORDER, MCALLS, PDESTS = _make_plan()
MAXOPS = max(len(o) for o in OPS)

SCRATCH = {
    "own_m": ("sbuf", [P, P], "bfloat16"),
    "own_t": ("sbuf", [P, P], "bfloat16"),
    "xs": ("sbuf", [P, F], "bfloat16"),
    "pin": ("sbuf", [P, F], "bfloat16"),
    "yb": ("sbuf", [P, F], "bfloat16"),
}
SEMAPHORES = ["ldm", "ldt", "ldx", "arp", "sent", "st"]
for _k in range(1, N - 1):
    SCRATCH["land%d" % _k] = ("sbuf", [P, P], "bfloat16")
    SEMAPHORES.append("arr%d" % _k)
for _i in range(MAXOPS):
    SCRATCH["u%d" % _i] = ("sbuf", [P, P], "bfloat16")
    SCRATCH["ps%d" % _i] = ("psum", [P, 512], "float32")
    SEMAPHORES.append("mm%d" % _i)
    SEMAPHORES.append("cp%d" % _i)


def _engines(topo, cores, src, dests, want):
    allowed = -1
    for d in dests:
        if not topo.may_write(cores[src], cores[d]):
            raise ValueError("rank %d may not write to rank %d" % (src, d))
        allowed &= topo.mask(cores[src], cores[d])
    mask = 0
    n = 0
    b = 0
    while n < want and (allowed >> b):
        if (allowed >> b) & 1:
            mask |= 1 << b
            n += 1
        b += 1
    return mask, n


def _send(g, T, topo, src, dests, want, buf, land, sem):
    mask, n = _engines(topo, T.cores, src, dests, want)
    ids = []
    for d in dests:
        rid, pid, _se = topo.addr(T.cores[d])
        ids.append(DstId(rid=rid, pnc=pid))
    g.remote_dma_fused(
        [RemoteDMATransfer(dst_ids=ids, dma_engine_mask=mask, remote_sem=sem,
                           srcs=[buf[:]], dsts=[land[:] for _d in dests], alu_op=0)],
        local_sem=T.sem.sent)
    return n


def rank_program(g, core, T, topo):
    r = T.rank_of(core)
    if r is None:
        return
    sem = T.sem
    forms_sent = [c[0] for c in MCALLS[r]]

    if r == 0:
        g.sync.dma_start(T.xs[:], T.x[:]).then_inc(sem.ldx, 16)
    elif "t" in forms_sent:
        g.sync.dma_start(T.own_t[:], T.mt[:]).then_inc(sem.ldt, 16)
    g.scalar.dma_start(T.own_m[:], T.m[:]).then_inc(sem.ldm, 16)

    sent = 0
    waited = []
    for fm, dests in MCALLS[r]:
        if fm not in waited:
            g.wait_ge(sem.ldt if fm == "t" else sem.ldm, 16)
            waited.append(fm)
        sent += _send(g, T, topo, r, dests, NE_M, T.own_t if fm == "t" else T.own_m,
                      T["land%d" % r], sem["arr%d" % r])

    lst = OPS[r]
    last = len(lst) - 1

    def out_of(i):
        if i == last:
            return T.yb[:]
        return T["u%d" % i][:, 0:lst[i][2]]

    def operand(d):
        if d[0] == "own":
            g.tensor.wait_ge(sem.ldm, 16)
            return T.own_m[:]
        if d[0] == "x":
            g.tensor.wait_ge(sem.ldx, 16)
            return T.xs[:]
        if d[0] == "pin":
            j = SRC[r]
            g.tensor.wait_ge(sem.arp, _engines(topo, T.cores, j, PDESTS[j], NE_P)[1])
            return T.pin[:]
        if d[0] == "land":
            k = d[1]
            for _fm, dests in MCALLS[k]:
                if r in dests:
                    g.tensor.wait_ge(sem["arr%d" % k], _engines(topo, T.cores, k, dests, NE_M)[1])
            return T["land%d" % k][:]
        g.tensor.wait_ge(sem["cp%d" % d[1]], 1)
        return out_of(d[1])

    for i in ORDER[r]:
        a, b, cols = lst[i]
        lhs = operand(a)
        rhs = operand(b)
        ps = T["ps%d" % i][:, 0:cols]
        g.tensor.matmul(ps, lhs, rhs, start=True, stop=True).then_inc(sem["mm%d" % i], 1)
        g.vector.wait_ge(sem["mm%d" % i], 1)
        g.vector.tensor_copy(out_of(i), ps).then_inc(sem["cp%d" % i], 1)

    g.sync.wait_ge(sem["cp%d" % last], 1)
    g.sync.dma_start(T.y[:], T.yb[:]).then_inc(sem.st, 16)
    if PDESTS[r]:
        g.wait_ge(sem["cp%d" % last], 1)
        sent += _send(g, T, topo, r, PDESTS[r], NE_P, T.yb, T.pin, sem.arp)
    if sent:
        g.wait_ge(sem.sent, sent)
    g.sync.wait_ge(sem.st, 16)
